import numpy as np
import ml_dtypes


def mxq(x, axis, fmt="e4m3"):
    dtype, down = {"e4m3": (ml_dtypes.float8_e4m3fn, 7), "e5m2": (ml_dtypes.float8_e5m2, 14)}[fmt]
    v = np.moveaxis(np.asarray(x, np.float32).astype(ml_dtypes.bfloat16).astype(np.float64), axis, -1)
    blocks = v.reshape(v.shape[:-1] + (-1, 32))
    amax = np.abs(blocks).max(-1, keepdims=True)
    byte = np.maximum(np.where(amax > 0, np.frexp(amax)[1] - 1 + 127, 0) - down, 1)
    scale = np.exp2(byte - 127.0)
    codes = (blocks / scale).astype(np.float32).astype(dtype).astype(np.float64)
    return np.moveaxis((codes * scale).reshape(v.shape), -1, axis)


WIDE = False


def mx_kscale(k):
    if not WIDE:
        return np.ones(k)
    levels = np.array([10, -10, 5, -5, 0])
    if k % 512:
        return np.exp2(np.random.permutation(np.resize(levels, k // 32))).repeat(32)
    a = np.empty((k // 512, 16))
    for p in range(k // 512):
        a[p, :8] = np.random.permutation(np.resize(levels, 8))
        for g in range(8):
            far = levels[np.abs(levels - a[p, g]) >= 10]
            a[p, g + 8] = far[np.random.randint(len(far))]
    return np.exp2(a.ravel()).repeat(32)


def f64(x):
    return np.asarray(x).astype(np.float64)


def striped(idx):
    return np.tile(idx.reshape(-1, 16).T, (8, 1)).astype(np.uint16)


def unstriped(offs):
    return offs[:16].T.reshape(-1).astype(np.int64)


def pack_weight(w):
    k, n = w.shape
    w = f64(np.asarray(w, np.float32).astype(ml_dtypes.bfloat16)).reshape(k // 32, 32, n)
    amax = np.abs(w).max(1)
    byte = np.clip(np.where(amax > 0, np.frexp(amax)[1] - 1 + 127 - 7, 1), 1, 254)
    scaled = (w * np.exp2(127.0 - byte)[:, None, :]).reshape(k, n).astype(np.float32)
    words = np.ascontiguousarray(scaled.reshape(k // 512, 128, 4, n).transpose(0, 1, 3, 2)).astype(ml_dtypes.float8_e4m3fn).view(np.uint8)
    return words, np.ascontiguousarray(byte.astype(np.uint8).reshape(k // 512, 16, n))


def unpack_weight(words, scales):
    g, p, n, _ = words.shape
    vals = np.ascontiguousarray(words).view(ml_dtypes.float8_e4m3fn).astype(np.float64) * np.repeat(np.exp2(scales.astype(np.float64) - 127.0), 8, axis=1)[..., None]
    return vals.transpose(0, 1, 3, 2).reshape(g * 512, n)


K, T, S, N, D, V = 512, 4096, 1024, 256, 4, 256


def setup_inputs():
    n = np.random.standard_normal
    s = mx_kscale(K)[:, None]
    packed_xT = pack_weight(n((K, T)) * s)
    return {
        "x_words": packed_xT[0],
        "x_scales": packed_xT[1],
        "w1": (n((K, N)) / np.sqrt(K) / s).astype(np.float32),
        "w2": (n((K, N)) / np.sqrt(K) / s).astype(np.float32),
        "steer": (np.random.uniform(0.5, 1.5, (N, V))).astype(np.float32),
        "mica": (n((N, V))).astype(np.float32),
        "micb": (n((N, V))).astype(np.float32),
        "offs": striped(np.random.permutation(T)[:S]),
    }


def reference(x_words, x_scales, w1, w2, steer, mica, micb, offs):
    xq = unpack_weight(x_words, x_scales)[:, unstriped(offs)]
    nb = mxq(f64(w2), 0, "e4m3").T @ xq
    bb = (nb) ** 2
    rb = bb.reshape(len(bb), -1, D).mean(axis=2) + 0.1
    na = mxq(f64(w1), 0, "e4m3").T @ xq
    ab = na * nb
    rx = ab.reshape(len(ab), -1, D).mean(axis=2)
    wa = rb - (rx * f64(steer))
    aa = (na) ** 2
    ra = aa.reshape(len(aa), -1, D).mean(axis=2) + 0.1
    wb = ra * f64(steer) - rx
    den = wa + wb * f64(steer)
    return (wa * f64(mica) + wb * f64(micb)) / (den + 0.05)

@@ -1,0 +1,186 @@
+from contextlib import ExitStack
+
+import concourse.mybir as mybir
+from concourse.masks import make_identity
+
+K, T, S, N, D, V = 512, 4096, 1024, 256, 4, 256
+FLOPS = 2 * 2 * K * S * N
+
+F32 = mybir.dt.float32
+BF16 = mybir.dt.bfloat16
+I32 = mybir.dt.int32
+U32 = mybir.dt.uint32
+U16 = mybir.dt.uint16
+U8 = mybir.dt.uint8
+FP8X4 = mybir.dt.float8_e4m3fn_x4
+ACT = mybir.ActivationFunctionType
+ALU = mybir.AluOpType
+
+P = 128
+PACK = 4
+HALVES = V // P
+BANDS = N // P
+HALF = D * P
+LIST_COLS = HALF // 16
+LOAD = 0.1 * D
+FIRST_WORDS = T // 4
+
+
+def tile_picked_ymvdr_beam_p_kernel(
+    tc, x_words, x_scales, w1, w2, steer, mica, micb, offs, out
+):
+    nc = tc.nc
+    with ExitStack() as ctx:
+        keep = ctx.enter_context(tc.tile_pool(name="keep", bufs=1))
+        work = ctx.enter_context(tc.tile_pool(name="work", bufs=4))
+        prod = ctx.enter_context(tc.psum_pool(name="prod", bufs=3))
+        summ = ctx.enter_context(tc.psum_pool(name="summ", bufs=2))
+
+        offsets = keep.tile([P, S // 16], U16, name="offsets")
+        nc.sync.dma_start(offsets[:], offs)
+
+        words = keep.tile([P, T], I32, name="words", align_bytes=64)
+        words_hbm = x_words[0].rearrange("p n t -> p (n t)").bitcast(I32)
+        nc.sync.dma_start(words[:, :FIRST_WORDS], words_hbm[:, :FIRST_WORDS])
+
+        scale_rows = keep.tile([P, T], U8, name="scale_rows", align_bytes=64)
+        nc.vector.memset(scale_rows[:].bitcast(I32), 0)
+        for q in range(4):
+            nc.sync.dma_start(
+                scale_rows[32 * q : 32 * q + 4, :].bitcast(I32),
+                x_scales[0, 4 * q : 4 * q + 4, :].bitcast(I32),
+            )
+        nc.sync.dma_start(words[:, FIRST_WORDS:], words_hbm[:, FIRST_WORDS:])
+
+        steer_sb = keep.tile([P, BANDS, V], F32, name="steer_sb")
+        nc.sync.dma_start(steer_sb[:], steer.rearrange("(t p) v -> p t v", p=P))
+
+        raw = []
+        for i, w in enumerate((w1, w2)):
+            w_raw = keep.tile([P, PACK, N], F32, name="w_raw%d" % i)
+            nc.sync.dma_start(w_raw[:], w.rearrange("(p j) c -> p j c", j=PACK))
+            raw.append(w_raw)
+
+        signal = keep.tile([P, 2, BANDS, V], F32, name="signal")
+        nc.sync.dma_start(signal[:, 0], mica.rearrange("(t p) v -> p t v", p=P))
+        micb_sb = keep.tile([P, BANDS, V], F32, name="micb_sb")
+        nc.sync.dma_start(micb_sb[:], micb.rearrange("(t p) v -> p t v", p=P))
+
+        ident = keep.tile([P, P], F32, name="ident")
+        make_identity(nc, ident[:])
+
+        picked_scales = keep.tile([P, S], U8, name="picked_scales", align_bytes=64)
+        nc.vector.tensor_copy(picked_scales[:], scale_rows[:].indirect(offsets[:]))
+        x_sc = keep.tile([P, S], U8, name="x_sc", align_bytes=64)
+        nc.vector.tensor_copy(
+            x_sc[:].rearrange("p (h d v) -> p h d v", h=HALVES, d=D),
+            picked_scales[:].rearrange("p (h v d) -> p h d v", h=HALVES, d=D),
+        )
+
+        x_cd = []
+        for h in range(HALVES):
+            codes = keep.tile([P, HALF], U32, name="x_cd%d" % h, align_bytes=64)
+            nc.vector.tensor_copy(
+                codes[:].rearrange("p (d v) -> p v d", d=D),
+                words[:].bitcast(U32).indirect(offsets[:, h * LIST_COLS : (h + 1) * LIST_COLS]),
+            )
+            x_cd.append(codes)
+
+        w_cd, w_sc = {}, {}
+        for t in range(BANDS):
+            for i in range(2):
+                grouped = keep.tile([P, P, PACK], BF16, name="grouped%d%d" % (i, t), align_bytes=64)
+                src = raw[i][:, :, t * P : (t + 1) * P].rearrange("p j c -> p c j")
+                if (t, i) == (0, 1):
+                    nc.vector.tensor_copy(grouped[:], src)
+                else:
+                    nc.scalar.copy(grouped[:], src)
+                w_cd[i, t] = keep.tile([P, P], U32, name="w_cd%d%d" % (i, t), align_bytes=64)
+                w_sc[i, t] = keep.tile([P, P], U8, name="w_sc%d%d" % (i, t), align_bytes=64)
+                nc.vector.quantize_mx(
+                    out=w_cd[i, t][:].bitcast(FP8X4),
+                    scales=w_sc[i, t][:],
+                    in_=grouped[:].rearrange("p c j -> p (c j)"),
+                )
+
+        def product(i, h, t):
+            bank = prod.tile([P, HALF], F32, name="mic%d" % i)
+            for d in range(D):
+                cols = slice(d * P, (d + 1) * P)
+                nc.tensor.matmul_mx(
+                    out=bank[:, cols],
+                    lhsT=x_cd[h][:, cols].bitcast(FP8X4),
+                    lhsT_scale=x_sc[:, h * HALF + d * P : h * HALF + (d + 1) * P],
+                    rhs=w_cd[i, t][:].bitcast(FP8X4),
+                    rhs_scale=w_sc[i, t][:],
+                    start=True,
+                    stop=True,
+                )
+            return bank
+
+        def sum_frames(dst, terms, load):
+            nc.tensor.matmul(dst, load, ident[:], start=True, stop=False, is_transpose=True)
+            for d in range(D):
+                nc.tensor.matmul(
+                    dst, terms[:, d * P : (d + 1) * P], ident[:], start=False, stop=(d == D - 1), is_transpose=True
+                )
+
+        turned = summ.tile([P, HALVES, BANDS, P], F32, name="sums")
+        for h in range(HALVES):
+            for t in range(BANDS):
+                nc.tensor.transpose(turned[:, h, t], steer_sb[:, t, h * P : (h + 1) * P], ident[:])
+        steer_t = keep.tile([P, HALVES, BANDS, P], F32, name="steer_t")
+        nc.scalar.copy(steer_t[:], turned[:])
+        load_w = keep.tile([P, HALVES, BANDS, P], F32, name="load_w")
+        nc.scalar.activation(load_w[:], steer_t[:], ACT.Copy, scale=LOAD)
+        steer_sq = keep.tile([P, HALVES, BANDS, P], F32, name="steer_sq")
+        nc.scalar.activation(steer_sq[:], steer_t[:], ACT.Square)
+        load_d = keep.tile([P, HALVES, BANDS, P], F32, name="load_d")
+        nc.scalar.activation(load_d[:], steer_sq[:], ACT.Copy, scale=LOAD, bias=LOAD)
+
+        steered_a = keep.tile([P, BANDS, V], F32, name="steered_a")
+        for t in range(BANDS):
+            nc.gpsimd.tensor_tensor(steered_a[:, t], steer_sb[:, t], signal[:, 0, t], ALU.mult)
+            nc.gpsimd.tensor_tensor(signal[:, 1, t], micb_sb[:, t], steered_a[:, t], ALU.subtract)
+
+        for t in range(BANDS):
+            for h in range(HALVES):
+                na = product(0, h, t)
+                nb = product(1, h, t)
+                sa = work.tile([P, HALF], F32, name="sa")
+                u = work.tile([P, HALF], F32, name="u")
+                ua = work.tile([P, HALF], F32, name="ua")
+                uu = work.tile([P, HALF], F32, name="uu")
+                nc.vector.tensor_tensor(
+                    sa[:].rearrange("p (d m) -> p d m", d=D),
+                    na[:].rearrange("p (d m) -> p d m", d=D),
+                    steer_t[:, h, t : t + 1].to_broadcast([P, D, P]),
+                    ALU.mult,
+                )
+                nc.vector.tensor_tensor(u[:], sa[:], nb[:], ALU.subtract)
+                last = t == BANDS - 1
+                if last:
+                    nc.vector.tensor_tensor(ua[:], na[:], u[:], ALU.mult)
+                else:
+                    na_sb = work.tile([P, HALF], F32, name="na_sb")
+                    nc.scalar.copy(na_sb[:], na[:])
+                    nc.gpsimd.tensor_tensor(ua[:], na_sb[:], u[:], ALU.mult)
+                nc.scalar.activation(uu[:], u[:], ACT.Square)
+
+                sums = summ.tile([P, 2, P], F32, name="sums")
+                sum_frames(sums[:, 0], uu, load_d[:, h, t])
+                sum_frames(sums[:, 1], ua, load_w[:, h, t])
+
+                cols = slice(h * P, (h + 1) * P)
+                root = work.tile([P, P], F32, name="root")
+                nc.scalar.activation(root[:], sums[:, 0], ACT.Abs_reciprocal_sqrt, bias=0.05 * D)
+                inv = work.tile([P, P], F32, name="inv")
+                nc.scalar.activation(inv[:], root[:], ACT.Square)
+                parts = work.tile([P, 2, P], F32, name="parts")
+                nc.vector.tensor_tensor(parts[:], sums[:], signal[:, :, t, cols], ALU.mult)
+                tail = nc.vector if last else nc.gpsimd
+                num = work.tile([P, P], F32, name="num")
+                tail.tensor_tensor(num[:], parts[:, 0], parts[:, 1], ALU.add)
+                res = work.tile([P, P], F32, name="res")
+                tail.tensor_tensor(res[:], num[:], inv[:], ALU.mult)
+                nc.sync.dma_start(out[t * P : (t + 1) * P, cols], res[:])

@@ -66,6 +66,10 @@ def tile_picked_ymvdr_beam_p_kernel(
         micb_sb = keep.tile([P, BANDS, V], F32, name="micb_sb")
         nc.sync.dma_start(micb_sb[:], micb.rearrange("(t p) v -> p t v", p=P))
 
+        warm = keep.tile([P, 2], F32, name="warm")
+        nc.gpsimd.memset(warm[:, 0:1], 1.0)
+        nc.scalar.activation(warm[:, 1:2], warm[:, 0:1], ACT.Abs_reciprocal_sqrt, bias=0.05 * D)
+
         ident = keep.tile([P, P], F32, name="ident")
         make_identity(nc, ident[:])
 

@@ -45,11 +45,7 @@ def tile_picked_ymvdr_beam_p_kernel(
 
         scale_rows = keep.tile([P, T], U8, name="scale_rows", align_bytes=64)
         nc.vector.memset(scale_rows[:].bitcast(I32), 0)
-        for q in range(4):
-            nc.sync.dma_start(
-                scale_rows[32 * q : 32 * q + 4, :].bitcast(I32),
-                x_scales[0, 4 * q : 4 * q + 4, :].bitcast(I32),
-            )
+        nc.sync.dma_start(scale_rows[4:P:8, :].bitcast(I32), x_scales[0].bitcast(I32))
         nc.sync.dma_start(words[:, FIRST_WORDS:], words_hbm[:, FIRST_WORDS:])
 
         steer_sb = keep.tile([P, BANDS, V], F32, name="steer_sb")
@@ -75,11 +71,15 @@ def tile_picked_ymvdr_beam_p_kernel(
 
         picked_scales = keep.tile([P, S], U8, name="picked_scales", align_bytes=64)
         nc.vector.tensor_copy(picked_scales[:], scale_rows[:].indirect(offsets[:]))
-        x_sc = keep.tile([P, S], U8, name="x_sc", align_bytes=64)
+        dealt = keep.tile([P, S], U8, name="dealt", align_bytes=64)
         nc.vector.tensor_copy(
-            x_sc[:].rearrange("p (h d v) -> p h d v", h=HALVES, d=D),
+            dealt[:].rearrange("p (h d v) -> p h d v", h=HALVES, d=D),
             picked_scales[:].rearrange("p (h v d) -> p h d v", h=HALVES, d=D),
         )
+        x_sc = keep.tile([P, S], U8, name="x_sc", align_bytes=64)
+        nc.vector.memset(x_sc[:].bitcast(I32), 0)
+        for i in range(4):
+            nc.scalar.dma_start(x_sc[i:P:32, :].bitcast(I32), dealt[8 * i + 4 : P : 32, :].bitcast(I32))
 
         x_cd = []
         for h in range(HALVES):
@@ -94,11 +94,12 @@ def tile_picked_ymvdr_beam_p_kernel(
         for t in range(BANDS):
             for i in range(2):
                 grouped = keep.tile([P, P, PACK], BF16, name="grouped%d%d" % (i, t), align_bytes=64)
-                src = raw[i][:, :, t * P : (t + 1) * P].rearrange("p j c -> p c j")
+                src = raw[i][:, :, t * P : (t + 1) * P].rearrange("p j (c e) -> p c j e", e=4)
+                dst = grouped[:].rearrange("p (c e) j -> p c j e", e=4)
                 if (t, i) == (0, 1):
-                    nc.vector.tensor_copy(grouped[:], src)
+                    nc.vector.tensor_copy(dst, src)
                 else:
-                    nc.scalar.copy(grouped[:], src)
+                    nc.scalar.copy(dst, src)
                 w_cd[i, t] = keep.tile([P, P], U32, name="w_cd%d%d" % (i, t), align_bytes=64)
                 w_sc[i, t] = keep.tile([P, P], U8, name="w_sc%d%d" % (i, t), align_bytes=64)
                 nc.vector.quantize_mx(

@@ -58,9 +58,9 @@ def tile_picked_ymvdr_beam_p_kernel(
             raw.append(w_raw)
 
         signal = keep.tile([P, 2, BANDS, V], F32, name="signal")
-        nc.sync.dma_start(signal[:, 0], mica.rearrange("(t p) v -> p t v", p=P))
         micb_sb = keep.tile([P, BANDS, V], F32, name="micb_sb")
         nc.sync.dma_start(micb_sb[:], micb.rearrange("(t p) v -> p t v", p=P))
+        nc.sync.dma_start(signal[:, 0], mica.rearrange("(t p) v -> p t v", p=P))
 
         warm = keep.tile([P, 2], F32, name="warm")
         nc.gpsimd.memset(warm[:, 0:1], 1.0)
@@ -172,17 +172,25 @@ def tile_picked_ymvdr_beam_p_kernel(
                     nc.gpsimd.tensor_tensor(ua[:], na_sb[:], u[:], ALU.mult)
                 nc.scalar.activation(uu[:], u[:], ACT.Square)
 
-                sums = summ.tile([P, 2, P], F32, name="sums")
-                sum_frames(sums[:, 0], uu, load_d[:, h, t])
-                sum_frames(sums[:, 1], ua, load_w[:, h, t])
-
                 cols = slice(h * P, (h + 1) * P)
                 root = work.tile([P, P], F32, name="root")
-                nc.scalar.activation(root[:], sums[:, 0], ACT.Abs_reciprocal_sqrt, bias=0.05 * D)
                 inv = work.tile([P, P], F32, name="inv")
-                nc.scalar.activation(inv[:], root[:], ACT.Square)
                 parts = work.tile([P, 2, P], F32, name="parts")
-                nc.vector.tensor_tensor(parts[:], sums[:], signal[:, :, t, cols], ALU.mult)
+                if last and h == HALVES - 1:
+                    den = summ.tile([P, P], F32, name="sums")
+                    wb = prod.tile([P, P], F32, name="mic1")
+                    sum_frames(den[:], uu, load_d[:, h, t])
+                    sum_frames(wb[:], ua, load_w[:, h, t])
+                    nc.scalar.activation(root[:], den[:], ACT.Abs_reciprocal_sqrt, bias=0.05 * D)
+                    nc.vector.tensor_tensor(parts[:, 1], wb[:], signal[:, 1, t, cols], ALU.mult)
+                    nc.vector.tensor_tensor(parts[:, 0], den[:], signal[:, 0, t, cols], ALU.mult)
+                else:
+                    sums = summ.tile([P, 2, P], F32, name="sums")
+                    sum_frames(sums[:, 0], uu, load_d[:, h, t])
+                    sum_frames(sums[:, 1], ua, load_w[:, h, t])
+                    nc.scalar.activation(root[:], sums[:, 0], ACT.Abs_reciprocal_sqrt, bias=0.05 * D)
+                    nc.vector.tensor_tensor(parts[:], sums[:], signal[:, :, t, cols], ALU.mult)
+                nc.scalar.activation(inv[:], root[:], ACT.Square)
                 tail = nc.vector if last else nc.gpsimd
                 num = work.tile([P, P], F32, name="num")
                 tail.tensor_tensor(num[:], parts[:, 0], parts[:, 1], ALU.add)

@@ -58,9 +58,9 @@ def tile_picked_ymvdr_beam_p_kernel(
             raw.append(w_raw)
 
         signal = keep.tile([P, 2, BANDS, V], F32, name="signal")
+        nc.sync.dma_start(signal[:, 0], mica.rearrange("(t p) v -> p t v", p=P))
         micb_sb = keep.tile([P, BANDS, V], F32, name="micb_sb")
         nc.sync.dma_start(micb_sb[:], micb.rearrange("(t p) v -> p t v", p=P))
-        nc.sync.dma_start(signal[:, 0], mica.rearrange("(t p) v -> p t v", p=P))
 
         warm = keep.tile([P, 2], F32, name="warm")
         nc.gpsimd.memset(warm[:, 0:1], 1.0)
@@ -136,19 +136,17 @@ def tile_picked_ymvdr_beam_p_kernel(
                 nc.tensor.transpose(turned[:, h, t], steer_sb[:, t, h * P : (h + 1) * P], ident[:])
         steer_t = keep.tile([P, HALVES, BANDS, P], F32, name="steer_t")
         nc.scalar.copy(steer_t[:], turned[:])
-        load_w = keep.tile([P, HALVES, BANDS, P], F32, name="load_w")
-        nc.scalar.activation(load_w[:], steer_t[:], ACT.Copy, scale=LOAD)
-        steer_sq = keep.tile([P, HALVES, BANDS, P], F32, name="steer_sq")
-        nc.scalar.activation(steer_sq[:], steer_t[:], ACT.Square)
-        load_d = keep.tile([P, HALVES, BANDS, P], F32, name="load_d")
-        nc.scalar.activation(load_d[:], steer_sq[:], ACT.Copy, scale=LOAD, bias=LOAD)
-
-        steered_a = keep.tile([P, BANDS, V], F32, name="steered_a")
-        for t in range(BANDS):
-            nc.gpsimd.tensor_tensor(steered_a[:, t], steer_sb[:, t], signal[:, 0, t], ALU.mult)
-            nc.gpsimd.tensor_tensor(signal[:, 1, t], micb_sb[:, t], steered_a[:, t], ALU.subtract)
 
         for t in range(BANDS):
+            load_w = keep.tile([P, HALVES, P], F32, name="load_w%d" % t)
+            steer_sq = keep.tile([P, HALVES, P], F32, name="steer_sq%d" % t)
+            load_d = keep.tile([P, HALVES, P], F32, name="load_d%d" % t)
+            nc.scalar.activation(steer_sq[:], steer_t[:, :, t], ACT.Square)
+            nc.scalar.activation(load_d[:], steer_sq[:], ACT.Copy, scale=LOAD, bias=LOAD)
+            nc.scalar.activation(load_w[:], steer_t[:, :, t], ACT.Copy, scale=LOAD)
+            steered_a = keep.tile([P, V], F32, name="steered_a%d" % t)
+            nc.gpsimd.tensor_tensor(steered_a[:], steer_sb[:, t], signal[:, 0, t], ALU.mult)
+            nc.gpsimd.tensor_tensor(signal[:, 1, t], micb_sb[:, t], steered_a[:], ALU.subtract)
             for h in range(HALVES):
                 na = product(0, h, t)
                 nb = product(1, h, t)
@@ -179,15 +177,15 @@ def tile_picked_ymvdr_beam_p_kernel(
                 if last and h == HALVES - 1:
                     den = summ.tile([P, P], F32, name="sums")
                     wb = prod.tile([P, P], F32, name="mic1")
-                    sum_frames(den[:], uu, load_d[:, h, t])
-                    sum_frames(wb[:], ua, load_w[:, h, t])
+                    sum_frames(den[:], uu, load_d[:, h])
+                    sum_frames(wb[:], ua, load_w[:, h])
                     nc.scalar.activation(root[:], den[:], ACT.Abs_reciprocal_sqrt, bias=0.05 * D)
                     nc.vector.tensor_tensor(parts[:, 1], wb[:], signal[:, 1, t, cols], ALU.mult)
                     nc.vector.tensor_tensor(parts[:, 0], den[:], signal[:, 0, t, cols], ALU.mult)
                 else:
                     sums = summ.tile([P, 2, P], F32, name="sums")
-                    sum_frames(sums[:, 0], uu, load_d[:, h, t])
-                    sum_frames(sums[:, 1], ua, load_w[:, h, t])
+                    sum_frames(sums[:, 0], uu, load_d[:, h])
+                    sum_frames(sums[:, 1], ua, load_w[:, h])
                     nc.scalar.activation(root[:], sums[:, 0], ACT.Abs_reciprocal_sqrt, bias=0.05 * D)
                     nc.vector.tensor_tensor(parts[:], sums[:], signal[:, :, t, cols], ALU.mult)
                 nc.scalar.activation(inv[:], root[:], ACT.Square)

from contextlib import ExitStack

import concourse.mybir as mybir
from concourse.masks import make_identity

K, T, S, N, D, V = 512, 4096, 1024, 256, 4, 256
FLOPS = 2 * 2 * K * S * N

F32 = mybir.dt.float32
BF16 = mybir.dt.bfloat16
I32 = mybir.dt.int32
U32 = mybir.dt.uint32
U16 = mybir.dt.uint16
U8 = mybir.dt.uint8
FP8X4 = mybir.dt.float8_e4m3fn_x4
ACT = mybir.ActivationFunctionType
ALU = mybir.AluOpType

P = 128
PACK = 4
HALVES = V // P
BANDS = N // P
HALF = D * P
LIST_COLS = HALF // 16
LOAD = 0.1 * D
FIRST_WORDS = T // 4


def tile_picked_ymvdr_beam_p_kernel(
    tc, x_words, x_scales, w1, w2, steer, mica, micb, offs, out
):
    nc = tc.nc
    with ExitStack() as ctx:
        keep = ctx.enter_context(tc.tile_pool(name="keep", bufs=1))
        work = ctx.enter_context(tc.tile_pool(name="work", bufs=4))
        prod = ctx.enter_context(tc.psum_pool(name="prod", bufs=3))
        summ = ctx.enter_context(tc.psum_pool(name="summ", bufs=2))

        offsets = keep.tile([P, S // 16], U16, name="offsets")
        nc.sync.dma_start(offsets[:], offs)

        words = keep.tile([P, T], I32, name="words", align_bytes=64)
        words_hbm = x_words[0].rearrange("p n t -> p (n t)").bitcast(I32)
        nc.sync.dma_start(words[:, :FIRST_WORDS], words_hbm[:, :FIRST_WORDS])

        scale_rows = keep.tile([P, T], U8, name="scale_rows", align_bytes=64)
        nc.vector.memset(scale_rows[:].bitcast(I32), 0)
        nc.sync.dma_start(scale_rows[4:P:8, :].bitcast(I32), x_scales[0].bitcast(I32))
        nc.sync.dma_start(words[:, FIRST_WORDS:], words_hbm[:, FIRST_WORDS:])

        steer_sb = keep.tile([P, BANDS, V], F32, name="steer_sb")
        nc.sync.dma_start(steer_sb[:], steer.rearrange("(t p) v -> p t v", p=P))

        raw = []
        for i, w in enumerate((w1, w2)):
            w_raw = keep.tile([P, PACK, N], F32, name="w_raw%d" % i)
            nc.sync.dma_start(w_raw[:], w.rearrange("(p j) c -> p j c", j=PACK))
            raw.append(w_raw)

        signal = keep.tile([P, 2, BANDS, V], F32, name="signal")
        nc.sync.dma_start(signal[:, 0], mica.rearrange("(t p) v -> p t v", p=P))
        micb_sb = keep.tile([P, BANDS, V], F32, name="micb_sb")
        nc.sync.dma_start(micb_sb[:], micb.rearrange("(t p) v -> p t v", p=P))

        warm = keep.tile([P, 2], F32, name="warm")
        nc.gpsimd.memset(warm[:, 0:1], 1.0)
        nc.scalar.activation(warm[:, 1:2], warm[:, 0:1], ACT.Abs_reciprocal_sqrt, bias=0.05 * D)

        ident = keep.tile([P, P], F32, name="ident")
        make_identity(nc, ident[:])

        picked_scales = keep.tile([P, S], U8, name="picked_scales", align_bytes=64)
        nc.vector.tensor_copy(picked_scales[:], scale_rows[:].indirect(offsets[:]))
        dealt = keep.tile([P, S], U8, name="dealt", align_bytes=64)
        nc.vector.tensor_copy(
            dealt[:].rearrange("p (h d v) -> p h d v", h=HALVES, d=D),
            picked_scales[:].rearrange("p (h v d) -> p h d v", h=HALVES, d=D),
        )
        x_sc = keep.tile([P, S], U8, name="x_sc", align_bytes=64)
        nc.vector.memset(x_sc[:].bitcast(I32), 0)
        for i in range(4):
            nc.scalar.dma_start(x_sc[i:P:32, :].bitcast(I32), dealt[8 * i + 4 : P : 32, :].bitcast(I32))

        x_cd = []
        for h in range(HALVES):
            codes = keep.tile([P, HALF], U32, name="x_cd%d" % h, align_bytes=64)
            nc.vector.tensor_copy(
                codes[:].rearrange("p (d v) -> p v d", d=D),
                words[:].bitcast(U32).indirect(offsets[:, h * LIST_COLS : (h + 1) * LIST_COLS]),
            )
            x_cd.append(codes)

        w_cd, w_sc = {}, {}
        for t in range(BANDS):
            for i in range(2):
                grouped = keep.tile([P, P, PACK], BF16, name="grouped%d%d" % (i, t), align_bytes=64)
                src = raw[i][:, :, t * P : (t + 1) * P].rearrange("p j (c e) -> p c j e", e=4)
                dst = grouped[:].rearrange("p (c e) j -> p c j e", e=4)
                if (t, i) == (0, 1):
                    nc.vector.tensor_copy(dst, src)
                else:
                    nc.scalar.copy(dst, src)
                w_cd[i, t] = keep.tile([P, P], U32, name="w_cd%d%d" % (i, t), align_bytes=64)
                w_sc[i, t] = keep.tile([P, P], U8, name="w_sc%d%d" % (i, t), align_bytes=64)
                nc.vector.quantize_mx(
                    out=w_cd[i, t][:].bitcast(FP8X4),
                    scales=w_sc[i, t][:],
                    in_=grouped[:].rearrange("p c j -> p (c j)"),
                )

        def product(i, h, t):
            bank = prod.tile([P, HALF], F32, name="mic%d" % i)
            for d in range(D):
                cols = slice(d * P, (d + 1) * P)
                nc.tensor.matmul_mx(
                    out=bank[:, cols],
                    lhsT=x_cd[h][:, cols].bitcast(FP8X4),
                    lhsT_scale=x_sc[:, h * HALF + d * P : h * HALF + (d + 1) * P],
                    rhs=w_cd[i, t][:].bitcast(FP8X4),
                    rhs_scale=w_sc[i, t][:],
                    start=True,
                    stop=True,
                )
            return bank

        def sum_frames(dst, terms, load):
            nc.tensor.matmul(dst, load, ident[:], start=True, stop=False, is_transpose=True)
            for d in range(D):
                nc.tensor.matmul(
                    dst, terms[:, d * P : (d + 1) * P], ident[:], start=False, stop=(d == D - 1), is_transpose=True
                )

        turned = summ.tile([P, HALVES, BANDS, P], F32, name="sums")
        for h in range(HALVES):
            for t in range(BANDS):
                nc.tensor.transpose(turned[:, h, t], steer_sb[:, t, h * P : (h + 1) * P], ident[:])
        steer_t = keep.tile([P, HALVES, BANDS, P], F32, name="steer_t")
        nc.scalar.copy(steer_t[:], turned[:])

        for t in range(BANDS):
            load_w = keep.tile([P, HALVES, P], F32, name="load_w%d" % t)
            steer_sq = keep.tile([P, HALVES, P], F32, name="steer_sq%d" % t)
            load_d = keep.tile([P, HALVES, P], F32, name="load_d%d" % t)
            nc.scalar.activation(steer_sq[:], steer_t[:, :, t], ACT.Square)
            nc.scalar.activation(load_d[:], steer_sq[:], ACT.Copy, scale=LOAD, bias=LOAD)
            nc.scalar.activation(load_w[:], steer_t[:, :, t], ACT.Copy, scale=LOAD)
            steered_a = keep.tile([P, V], F32, name="steered_a%d" % t)
            nc.gpsimd.tensor_tensor(steered_a[:], steer_sb[:, t], signal[:, 0, t], ALU.mult)
            nc.gpsimd.tensor_tensor(signal[:, 1, t], micb_sb[:, t], steered_a[:], ALU.subtract)
            for h in range(HALVES):
                na = product(0, h, t)
                nb = product(1, h, t)
                sa = work.tile([P, HALF], F32, name="sa")
                u = work.tile([P, HALF], F32, name="u")
                ua = work.tile([P, HALF], F32, name="ua")
                uu = work.tile([P, HALF], F32, name="uu")
                nc.vector.tensor_tensor(
                    sa[:].rearrange("p (d m) -> p d m", d=D),
                    na[:].rearrange("p (d m) -> p d m", d=D),
                    steer_t[:, h, t : t + 1].to_broadcast([P, D, P]),
                    ALU.mult,
                )
                nc.vector.tensor_tensor(u[:], sa[:], nb[:], ALU.subtract)
                last = t == BANDS - 1
                if last:
                    nc.vector.tensor_tensor(ua[:], na[:], u[:], ALU.mult)
                else:
                    na_sb = work.tile([P, HALF], F32, name="na_sb")
                    nc.scalar.copy(na_sb[:], na[:])
                    nc.gpsimd.tensor_tensor(ua[:], na_sb[:], u[:], ALU.mult)
                nc.scalar.activation(uu[:], u[:], ACT.Square)

                cols = slice(h * P, (h + 1) * P)
                root = work.tile([P, P], F32, name="root")
                inv = work.tile([P, P], F32, name="inv")
                parts = work.tile([P, 2, P], F32, name="parts")
                if last and h == HALVES - 1:
                    den = summ.tile([P, P], F32, name="sums")
                    wb = prod.tile([P, P], F32, name="mic1")
                    sum_frames(den[:], uu, load_d[:, h])
                    sum_frames(wb[:], ua, load_w[:, h])
                    nc.scalar.activation(root[:], den[:], ACT.Abs_reciprocal_sqrt, bias=0.05 * D)
                    nc.vector.tensor_tensor(parts[:, 1], wb[:], signal[:, 1, t, cols], ALU.mult)
                    nc.vector.tensor_tensor(parts[:, 0], den[:], signal[:, 0, t, cols], ALU.mult)
                else:
                    sums = summ.tile([P, 2, P], F32, name="sums")
                    sum_frames(sums[:, 0], uu, load_d[:, h])
                    sum_frames(sums[:, 1], ua, load_w[:, h])
                    nc.scalar.activation(root[:], sums[:, 0], ACT.Abs_reciprocal_sqrt, bias=0.05 * D)
                    nc.vector.tensor_tensor(parts[:], sums[:], signal[:, :, t, cols], ALU.mult)
                nc.scalar.activation(inv[:], root[:], ACT.Square)
                tail = nc.vector if last else nc.gpsimd
                num = work.tile([P, P], F32, name="num")
                tail.tensor_tensor(num[:], parts[:, 0], parts[:, 1], ALU.add)
                res = work.tile([P, P], F32, name="res")
                tail.tensor_tensor(res[:], num[:], inv[:], ALU.mult)
                nc.sync.dma_start(out[t * P : (t + 1) * P, cols], res[:])
